import numpy as np
import ml_dtypes


def mxq(x, axis, fmt="e4m3"):
    dtype, down = {"e4m3": (ml_dtypes.float8_e4m3fn, 7), "e5m2": (ml_dtypes.float8_e5m2, 14)}[fmt]
    v = np.moveaxis(np.asarray(x, np.float32).astype(ml_dtypes.bfloat16).astype(np.float64), axis, -1)
    blocks = v.reshape(v.shape[:-1] + (-1, 32))
    amax = np.abs(blocks).max(-1, keepdims=True)
    byte = np.maximum(np.where(amax > 0, np.frexp(amax)[1] - 1 + 127, 0) - down, 1)
    scale = np.exp2(byte - 127.0)
    codes = (blocks / scale).astype(np.float32).astype(dtype).astype(np.float64)
    return np.moveaxis((codes * scale).reshape(v.shape), -1, axis)


WIDE = False


def mx_kscale(k, group=512):
    if not WIDE:
        return np.ones(k)
    levels = np.array([18, -18])
    if group != 512:
        return np.exp2(np.random.permutation(np.resize(levels, k // group))).repeat(group)
    if k % 512:
        return np.exp2(np.random.permutation(np.resize(levels, k // 32))).repeat(32)
    a = np.empty((k // 512, 16))
    for p in range(k // 512):
        a[p, :8] = np.random.permutation(np.resize(levels, 8))
        for g in range(8):
            far = levels[np.abs(levels - a[p, g]) >= 10]
            a[p, g + 8] = far[np.random.randint(len(far))]
    return np.exp2(a.ravel()).repeat(32)


def f64(x):
    return np.asarray(x).astype(np.float64)


def bf(x):
    return np.asarray(x, np.float32).astype(ml_dtypes.bfloat16)


def planes(Y):
    r, m = Y.shape
    b = f64(bf(Y)).reshape(r // 32, 32, m)
    amax = np.abs(b).max(1)
    byte = np.clip(np.where(amax > 0, np.frexp(amax)[1] - 1 + 127 - 7, 1), 1, 254)
    codes = (b * np.exp2(127.0 - byte)[:, None, :]).reshape(r, m).astype(np.float32).astype(ml_dtypes.float8_e4m3fn).view(np.uint8)
    words = codes.reshape(r // 512, 128, 4, m).transpose(0, 1, 3, 2)
    return np.ascontiguousarray(words), np.ascontiguousarray(byte.astype(np.uint8).reshape(r // 512, 16, m))


G, D, M, N, L = 4, 128, 128, 512, 768


def setup_inputs():
    n = np.random.standard_normal
    s_d = mx_kscale(D, 0)
    return {
        "x": (n((G, D, L)) * s_d[:, None]).astype(np.float32),
        "w0": (n((G, D, M)) / np.sqrt(3 * D) / s_d[:, None]).astype(np.float32),
        "w1": (n((G, D, M)) / np.sqrt(3 * D) / s_d[:, None]).astype(np.float32),
        "w2": (n((G, D, M)) / np.sqrt(3 * D) / s_d[:, None]).astype(np.float32),
        "b": (0.5 * n((G, M, 1))).astype(np.float32),
    }


def reference(x, w0, w1, w2, b):
    w0q = mxq(f64(w0), 1, "e4m3")
    xq = mxq(f64(x), 1, "e4m3")
    w1q = mxq(f64(w1), 1, "e4m3")
    w2q = mxq(f64(w2), 1, "e4m3")
    z = (w0q.transpose(0, 2, 1) @ xq[..., :512]) + (w1q.transpose(0, 2, 1) @ xq[..., 128 : 640]) + (w2q.transpose(0, 2, 1) @ xq[..., 256 : 768])
    y = np.maximum(z + f64(b), 0.0)
    Y = y.reshape(G * M, N)
    words, scales = planes(Y)
    return Y, words, scales

@@ -1,0 +1,184 @@
+from contextlib import ExitStack
+
+import concourse.mybir as mybir
+
+G, D, M, N, L = 4, 128, 128, 512, 768
+TAPS = 3
+FLOPS = 2 * G * TAPS * D * M * N
+
+F32 = mybir.dt.float32
+BF16 = mybir.dt.bfloat16
+U32 = mybir.dt.uint32
+I32 = mybir.dt.int32
+U8 = mybir.dt.uint8
+FP8X4 = mybir.dt.float8_e4m3fn_x4
+ACT = mybir.ActivationFunctionType
+ALU = mybir.AluOpType
+
+P = 128
+PACK = 4
+ROWS = 32
+CHUNK = 128
+HALF = 256
+X_FIRST = 512
+X_VECTOR = 344
+PLANE_VECTOR = 168
+
+
+def walk_out(t, c0, c1):
+    return t[:, c0:c1, :].rearrange("p (c i) t -> p c t i", i=4)
+
+
+def walk_in(t, c0, c1):
+    return t[:, :, c0:c1].rearrange("p t (c i) -> p c t i", i=4)
+
+
+def tile_rows_pl_conv_relu_kernel(tc, x, w0, w1, w2, b, out_0, out_1, out_2):
+    nc = tc.nc
+    x_rows = x.rearrange("g (p j) l -> (g p) j l", j=PACK)
+    w_rows = [w.rearrange("g (p j) m -> (g p) j m", j=PACK) for w in (w0, w1, w2)]
+    y_rows = out_0.rearrange("(g m) n -> m g n", g=G)
+    words_hbm = out_1.rearrange("s p n u -> (s p) (n u)").bitcast(I32)
+    scales_hbm = out_2.rearrange("s f n -> (s f) n").bitcast(I32)
+
+    with ExitStack() as ctx:
+        pool = ctx.enter_context(tc.tile_pool(name="sb", bufs=1))
+        psum = ctx.enter_context(tc.psum_pool(name="ps", bufs=1))
+        ctx.enter_context(tc.manual_schedule())
+
+        def sb(name, shape, dtype):
+            return pool.tile(shape, dtype, name=name, align_bytes=64)
+
+        x_width = (X_FIRST, L - X_FIRST)
+        x_raw = [sb("x_raw%d" % h, [P, PACK, x_width[h]], F32) for h in range(2)]
+        x_bf = [sb("x_bf%d" % h, [P, x_width[h], PACK], BF16) for h in range(2)]
+        x_codes = [sb("x_codes%d" % h, [P, x_width[h]], U32) for h in range(2)]
+        x_scales = [sb("x_scales%d" % h, [P, x_width[h]], U8) for h in range(2)]
+        w_raw = [sb("w_raw%d" % t, [P, PACK, M], F32) for t in range(TAPS)]
+        w_bf = [sb("w_bf%d" % t, [P, M, PACK], BF16) for t in range(TAPS)]
+        w_codes = [sb("w_codes%d" % t, [P, M], U32) for t in range(TAPS)]
+        w_scales = [sb("w_scales%d" % t, [P, M], U8) for t in range(TAPS)]
+        b_rows = sb("b_rows", [P, G * ROWS], F32)
+        b_cols = sb("b_cols", [P, G * ROWS], F32)
+        acc = [[psum.tile([P, HALF], F32, name="acc%d_%d" % (h, g)) for g in range(G)] for h in range(2)]
+        y32 = [[sb("y32_%d_%d" % (h, a), [P, 2, HALF], F32) for a in range(2)] for h in range(2)]
+        y16 = [[sb("y16_%d_%d" % (h, g), [P, HALF], BF16) for g in range(G)] for h in range(2)]
+        y_rows4 = [sb("y_rows4_%d" % h, [P, PACK, HALF], BF16) for h in range(2)]
+        y_bf = [sb("y_bf%d" % h, [P, HALF, PACK], BF16) for h in range(2)]
+        y_codes = [sb("y_codes%d" % h, [P, HALF], U32) for h in range(2)]
+        y_scales = sb("y_scales", [P, N], U8)
+
+        def quantize(codes, scales, grouped):
+            nc.vector.quantize_mx(
+                out=codes.bitcast(FP8X4), scales=scales, in_=grouped.rearrange("p w j -> p (w j)")
+            )
+
+        def cast_vector(dst, src, c0, c1):
+            nc.vector.tensor_copy(out=walk_out(dst, c0, c1), in_=walk_in(src, c0, c1))
+
+        def cast_scalar(dst, src, c0, c1):
+            nc.scalar.activation(out=walk_out(dst, c0, c1), in_=walk_in(src, c0, c1), func=ACT.Copy)
+
+        def tap(j, t):
+            h, c = j // 2, j + t
+            xh = 0 if c * CHUNK < X_FIRST else 1
+            c0 = c * CHUNK - xh * X_FIRST
+            for g in range(G):
+                rows = slice(ROWS * g, ROWS * (g + 1))
+                nc.tensor.matmul_mx(
+                    out=acc[h][g][:, (j % 2) * CHUNK : (j % 2 + 1) * CHUNK],
+                    lhsT=w_codes[t][rows, :].bitcast(FP8X4),
+                    lhsT_scale=w_scales[t][rows, :],
+                    rhs=x_codes[xh][rows, c0 : c0 + CHUNK].bitcast(FP8X4),
+                    rhs_scale=x_scales[xh][rows, c0 : c0 + CHUNK],
+                    start=(t == 0),
+                    stop=(t == TAPS - 1),
+                )
+
+        def relu_scalar(dst, h, g):
+            nc.scalar.activation(
+                out=dst, in_=acc[h][g][:], func=ACT.Relu, bias=b_cols[:, ROWS * g : ROWS * g + 1]
+            )
+
+        def relu_vector(dst, h, g):
+            nc.vector.tensor_scalar(
+                out=dst, in0=acc[h][g][:], scalar1=b_cols[:, ROWS * g : ROWS * g + 1], scalar2=0.0,
+                op0=ALU.add, op1=ALU.max,
+            )
+
+        def regroup(h, g):
+            nc.sync.dma_start(out=y_rows4[h][ROWS * g : ROWS * (g + 1), :, :], in_=y16[h][g][:])
+
+        def store_y(h, a):
+            nc.sync.dma_start(out=y_rows[:, 2 * a : 2 * a + 2, h * HALF : (h + 1) * HALF], in_=y32[h][a][:])
+
+        def store_words(h):
+            nc.sync.dma_start(out=words_hbm[:, h * HALF : (h + 1) * HALF], in_=y_codes[h][:].bitcast(I32))
+
+        nc.sync.dma_start(out=x_raw[0][:], in_=x_rows[:, :, 0:X_FIRST])
+        for t in range(TAPS):
+            nc.sync.dma_start(out=w_raw[t][:], in_=w_rows[t])
+        nc.sync.dma_start(out=x_raw[1][:], in_=x_rows[:, :, X_FIRST:L])
+
+        nc.vector.memset(b_rows[:], 0.0)
+        nc.scalar.dma_start(
+            out=b_rows[0:P:ROWS, :].rearrange("a (g i) -> a g i", g=G),
+            in_=b.rearrange("g (a i) o -> a g (i o)", i=ROWS),
+        )
+        nc.vector.transpose(out=b_cols[:], in_=b_rows[:])
+
+        cast_scalar(x_bf[0], x_raw[0], X_VECTOR, X_FIRST)
+        cast_vector(x_bf[0], x_raw[0], 0, HALF)
+        cast_vector(x_bf[0], x_raw[0], HALF, X_VECTOR)
+        cast_scalar(w_bf[0], w_raw[0], 0, M)
+        cast_scalar(w_bf[1], w_raw[1], 0, M)
+        quantize(x_codes[0][:, 0:HALF], x_scales[0][:, 0:HALF], x_bf[0][:, 0:HALF, :])
+        quantize(x_codes[0][:, HALF:X_FIRST], x_scales[0][:, HALF:X_FIRST], x_bf[0][:, HALF:X_FIRST, :])
+        quantize(w_codes[0][:], w_scales[0][:], w_bf[0][:])
+        tap(0, 0)
+        tap(2, 0)
+        cast_vector(w_bf[2], w_raw[2], 0, M)
+        quantize(w_codes[1][:], w_scales[1][:], w_bf[1][:])
+        tap(0, 1)
+        tap(2, 1)
+        quantize(w_codes[2][:], w_scales[2][:], w_bf[2][:])
+        tap(0, 2)
+        for t in range(TAPS):
+            tap(1, t)
+
+        cast_vector(x_bf[1], x_raw[1], 0, HALF)
+        for g in range(G):
+            relu_scalar(y16[0][g][:], 0, g)
+            regroup(0, g)
+        quantize(x_codes[1][:], x_scales[1][:], x_bf[1][:])
+        tap(2, 2)
+        for t in range(TAPS):
+            tap(3, t)
+        for g in (0, 1):
+            relu_scalar(y32[0][0][:, g, :], 0, g)
+        for g in (2, 3):
+            relu_vector(y32[0][1][:, g - 2, :], 0, g)
+        store_y(0, 0)
+
+        for g in (0, 1):
+            relu_scalar(y16[1][g][:], 1, g)
+            relu_vector(y16[1][g + 2][:], 1, g + 2)
+            regroup(1, g)
+            regroup(1, g + 2)
+        store_y(0, 1)
+        cast_vector(y_bf[0], y_rows4[0], 0, HALF)
+        for g in range(G):
+            relu_scalar(y32[1][g // 2][:, g % 2, :], 1, g)
+            if g % 2 == 1:
+                store_y(1, g // 2)
+        quantize(y_codes[0][:], y_scales[:, 0:HALF], y_bf[0][:])
+        store_words(0)
+        cast_vector(y_bf[1], y_rows4[1], 0, PLANE_VECTOR)
+        nc.scalar.copy(out=walk_out(y_bf[1], PLANE_VECTOR, HALF), in_=walk_in(y_rows4[1], PLANE_VECTOR, HALF))
+        quantize(y_codes[1][:], y_scales[:, HALF:N], y_bf[1][:])
+        store_words(1)
+        for q in range(G):
+            queue = nc.scalar if q % 2 == 0 else nc.sync
+            queue.dma_start(
+                out=scales_hbm[4 * q : 4 * q + 4, :], in_=y_scales[ROWS * q : ROWS * q + 4, :].bitcast(I32)
+            )

@@ -20,9 +20,11 @@ PACK = 4
 ROWS = 32
 CHUNK = 128
 HALF = 256
-X_FIRST = 512
+X_PARTS = ((0, 512), (512, 640), (640, 768))
 X_VECTOR = 344
-PLANE_VECTOR = 168
+MIDDLE_VECTOR = 32
+LAST_VECTOR = 80
+PLANE_VECTOR = 144
 
 
 def walk_out(t, c0, c1):
@@ -37,7 +39,6 @@ def tile_rows_pl_conv_relu_kernel(tc, x, w0, w1, w2, b, out_0, out_1, out_2):
     nc = tc.nc
     x_rows = x.rearrange("g (p j) l -> (g p) j l", j=PACK)
     w_rows = [w.rearrange("g (p j) m -> (g p) j m", j=PACK) for w in (w0, w1, w2)]
-    y_rows = out_0.rearrange("(g m) n -> m g n", g=G)
     words_hbm = out_1.rearrange("s p n u -> (s p) (n u)").bitcast(I32)
     scales_hbm = out_2.rearrange("s f n -> (s f) n").bitcast(I32)
 
@@ -49,11 +50,11 @@ def tile_rows_pl_conv_relu_kernel(tc, x, w0, w1, w2, b, out_0, out_1, out_2):
         def sb(name, shape, dtype):
             return pool.tile(shape, dtype, name=name, align_bytes=64)
 
-        x_width = (X_FIRST, L - X_FIRST)
-        x_raw = [sb("x_raw%d" % h, [P, PACK, x_width[h]], F32) for h in range(2)]
-        x_bf = [sb("x_bf%d" % h, [P, x_width[h], PACK], BF16) for h in range(2)]
-        x_codes = [sb("x_codes%d" % h, [P, x_width[h]], U32) for h in range(2)]
-        x_scales = [sb("x_scales%d" % h, [P, x_width[h]], U8) for h in range(2)]
+        x_width = [l1 - l0 for l0, l1 in X_PARTS]
+        x_raw = [sb("x_raw%d" % a, [P, PACK, wd], F32) for a, wd in enumerate(x_width)]
+        x_bf = [sb("x_bf%d" % a, [P, wd, PACK], BF16) for a, wd in enumerate(x_width)]
+        x_codes = [sb("x_codes%d" % a, [P, wd], U32) for a, wd in enumerate(x_width)]
+        x_scales = [sb("x_scales%d" % a, [P, wd], U8) for a, wd in enumerate(x_width)]
         w_raw = [sb("w_raw%d" % t, [P, PACK, M], F32) for t in range(TAPS)]
         w_bf = [sb("w_bf%d" % t, [P, M, PACK], BF16) for t in range(TAPS)]
         w_codes = [sb("w_codes%d" % t, [P, M], U32) for t in range(TAPS)]
@@ -61,7 +62,7 @@ def tile_rows_pl_conv_relu_kernel(tc, x, w0, w1, w2, b, out_0, out_1, out_2):
         b_rows = sb("b_rows", [P, G * ROWS], F32)
         b_cols = sb("b_cols", [P, G * ROWS], F32)
         acc = [[psum.tile([P, HALF], F32, name="acc%d_%d" % (h, g)) for g in range(G)] for h in range(2)]
-        y32 = [[sb("y32_%d_%d" % (h, a), [P, 2, HALF], F32) for a in range(2)] for h in range(2)]
+        y32 = [sb("y32_%d" % g, [P, N], F32) for g in range(G)]
         y16 = [[sb("y16_%d_%d" % (h, g), [P, HALF], BF16) for g in range(G)] for h in range(2)]
         y_rows4 = [sb("y_rows4_%d" % h, [P, PACK, HALF], BF16) for h in range(2)]
         y_bf = [sb("y_bf%d" % h, [P, HALF, PACK], BF16) for h in range(2)]
@@ -73,24 +74,33 @@ def tile_rows_pl_conv_relu_kernel(tc, x, w0, w1, w2, b, out_0, out_1, out_2):
                 out=codes.bitcast(FP8X4), scales=scales, in_=grouped.rearrange("p w j -> p (w j)")
             )
 
-        def cast_vector(dst, src, c0, c1):
+        def quantize_x(a, c0, c1):
+            quantize(x_codes[a][:, c0:c1], x_scales[a][:, c0:c1], x_bf[a][:, c0:c1, :])
+
+        def quantize_w(t):
+            quantize(w_codes[t][:], w_scales[t][:], w_bf[t][:])
+
+        def quantize_y(h):
+            quantize(y_codes[h][:], y_scales[:, h * HALF : (h + 1) * HALF], y_bf[h][:])
+
+        def group_vector(dst, src, c0, c1):
             nc.vector.tensor_copy(out=walk_out(dst, c0, c1), in_=walk_in(src, c0, c1))
 
-        def cast_scalar(dst, src, c0, c1):
+        def group_scalar(dst, src, c0, c1):
             nc.scalar.activation(out=walk_out(dst, c0, c1), in_=walk_in(src, c0, c1), func=ACT.Copy)
 
         def tap(j, t):
-            h, c = j // 2, j + t
-            xh = 0 if c * CHUNK < X_FIRST else 1
-            c0 = c * CHUNK - xh * X_FIRST
+            h, l0 = j // 2, (j + t) * CHUNK
+            a = max(a for a in range(len(X_PARTS)) if X_PARTS[a][0] <= l0)
+            c0 = l0 - X_PARTS[a][0]
             for g in range(G):
                 rows = slice(ROWS * g, ROWS * (g + 1))
                 nc.tensor.matmul_mx(
                     out=acc[h][g][:, (j % 2) * CHUNK : (j % 2 + 1) * CHUNK],
                     lhsT=w_codes[t][rows, :].bitcast(FP8X4),
                     lhsT_scale=w_scales[t][rows, :],
-                    rhs=x_codes[xh][rows, c0 : c0 + CHUNK].bitcast(FP8X4),
-                    rhs_scale=x_scales[xh][rows, c0 : c0 + CHUNK],
+                    rhs=x_codes[a][rows, c0 : c0 + CHUNK].bitcast(FP8X4),
+                    rhs_scale=x_scales[a][rows, c0 : c0 + CHUNK],
                     start=(t == 0),
                     stop=(t == TAPS - 1),
                 )
@@ -106,76 +116,92 @@ def tile_rows_pl_conv_relu_kernel(tc, x, w0, w1, w2, b, out_0, out_1, out_2):
                 op0=ALU.add, op1=ALU.max,
             )
 
-        def regroup(h, g):
-            nc.sync.dma_start(out=y_rows4[h][ROWS * g : ROWS * (g + 1), :, :], in_=y16[h][g][:])
+        def y32_half(h, g):
+            return y32[g][:, h * HALF : (h + 1) * HALF]
 
-        def store_y(h, a):
-            nc.sync.dma_start(out=y_rows[:, 2 * a : 2 * a + 2, h * HALF : (h + 1) * HALF], in_=y32[h][a][:])
+        def regroup(queue, h, g):
+            queue.dma_start(out=y_rows4[h][ROWS * g : ROWS * (g + 1), :, :], in_=y16[h][g][:])
+
+        def store_y(g):
+            nc.sync.dma_start(out=out_0[M * g : M * (g + 1), :], in_=y32[g][:])
 
         def store_words(h):
             nc.sync.dma_start(out=words_hbm[:, h * HALF : (h + 1) * HALF], in_=y_codes[h][:].bitcast(I32))
 
-        nc.sync.dma_start(out=x_raw[0][:], in_=x_rows[:, :, 0:X_FIRST])
-        for t in range(TAPS):
-            nc.sync.dma_start(out=w_raw[t][:], in_=w_rows[t])
-        nc.sync.dma_start(out=x_raw[1][:], in_=x_rows[:, :, X_FIRST:L])
+        def load_x(a):
+            nc.sync.dma_start(out=x_raw[a][:], in_=x_rows[:, :, X_PARTS[a][0] : X_PARTS[a][1]])
 
+        load_x(0)
         nc.vector.memset(b_rows[:], 0.0)
-        nc.scalar.dma_start(
+        nc.sync.dma_start(
             out=b_rows[0:P:ROWS, :].rearrange("a (g i) -> a g i", g=G),
             in_=b.rearrange("g (a i) o -> a g (i o)", i=ROWS),
         )
-        nc.vector.transpose(out=b_cols[:], in_=b_rows[:])
+        for t in range(TAPS):
+            nc.sync.dma_start(out=w_raw[t][:], in_=w_rows[t])
+        load_x(1)
+        load_x(2)
 
-        cast_scalar(x_bf[0], x_raw[0], X_VECTOR, X_FIRST)
-        cast_vector(x_bf[0], x_raw[0], 0, HALF)
-        cast_vector(x_bf[0], x_raw[0], HALF, X_VECTOR)
-        cast_scalar(w_bf[0], w_raw[0], 0, M)
-        cast_scalar(w_bf[1], w_raw[1], 0, M)
-        quantize(x_codes[0][:, 0:HALF], x_scales[0][:, 0:HALF], x_bf[0][:, 0:HALF, :])
-        quantize(x_codes[0][:, HALF:X_FIRST], x_scales[0][:, HALF:X_FIRST], x_bf[0][:, HALF:X_FIRST, :])
-        quantize(w_codes[0][:], w_scales[0][:], w_bf[0][:])
+        group_scalar(x_bf[0], x_raw[0], X_VECTOR, x_width[0])
+        group_vector(x_bf[0], x_raw[0], 0, HALF)
+        group_vector(x_bf[0], x_raw[0], HALF, X_VECTOR)
+        group_scalar(w_bf[0], w_raw[0], 0, M)
+        group_scalar(w_bf[1], w_raw[1], 0, M)
+        quantize_x(0, 0, HALF)
+        quantize_x(0, HALF, x_width[0])
+        quantize_w(0)
         tap(0, 0)
         tap(2, 0)
-        cast_vector(w_bf[2], w_raw[2], 0, M)
-        quantize(w_codes[1][:], w_scales[1][:], w_bf[1][:])
+        group_vector(w_bf[2], w_raw[2], 0, M)
+        quantize_w(1)
         tap(0, 1)
         tap(2, 1)
-        quantize(w_codes[2][:], w_scales[2][:], w_bf[2][:])
+        quantize_w(2)
         tap(0, 2)
         for t in range(TAPS):
             tap(1, t)
 
-        cast_vector(x_bf[1], x_raw[1], 0, HALF)
-        for g in range(G):
-            relu_scalar(y16[0][g][:], 0, g)
-            regroup(0, g)
-        quantize(x_codes[1][:], x_scales[1][:], x_bf[1][:])
+        group_vector(x_bf[1], x_raw[1], 0, MIDDLE_VECTOR)
+        group_scalar(x_bf[1], x_raw[1], MIDDLE_VECTOR, CHUNK)
+        nc.vector.transpose(out=b_cols[:], in_=b_rows[:])
+        quantize_x(1, 0, CHUNK)
         tap(2, 2)
-        for t in range(TAPS):
-            tap(3, t)
-        for g in (0, 1):
-            relu_scalar(y32[0][0][:, g, :], 0, g)
-        for g in (2, 3):
-            relu_vector(y32[0][1][:, g - 2, :], 0, g)
-        store_y(0, 0)
+        tap(3, 0)
+        tap(3, 1)
 
+        group_vector(x_bf[2], x_raw[2], 0, LAST_VECTOR)
+        group_scalar(x_bf[2], x_raw[2], LAST_VECTOR, CHUNK)
+        quantize_x(2, 0, CHUNK)
+        tap(3, 2)
         for g in (0, 1):
-            relu_scalar(y16[1][g][:], 1, g)
-            relu_vector(y16[1][g + 2][:], 1, g + 2)
-            regroup(1, g)
-            regroup(1, g + 2)
-        store_y(0, 1)
-        cast_vector(y_bf[0], y_rows4[0], 0, HALF)
-        for g in range(G):
-            relu_scalar(y32[1][g // 2][:, g % 2, :], 1, g)
-            if g % 2 == 1:
-                store_y(1, g // 2)
-        quantize(y_codes[0][:], y_scales[:, 0:HALF], y_bf[0][:])
+            relu_scalar(y16[0][g][:], 0, g)
+            regroup(nc.sync, 0, g)
+        relu_vector(y16[0][3][:], 0, 3)
+        regroup(nc.sync, 0, 3)
+        relu_scalar(y16[0][2][:], 0, 2)
+        regroup(nc.sync, 0, 2)
+
+        relu_scalar(y16[1][0][:], 1, 0)
+        relu_vector(y16[1][1][:], 1, 1)
+        regroup(nc.sync, 1, 0)
+        regroup(nc.sync, 1, 1)
+        relu_scalar(y16[1][2][:], 1, 2)
+        relu_vector(y16[1][3][:], 1, 3)
+        regroup(nc.scalar, 1, 2)
+        regroup(nc.sync, 1, 3)
+        for g in (0, 2):
+            for h in range(2):
+                relu_scalar(y32_half(h, g), h, g)
+                relu_vector(y32_half(h, g + 1), h, g + 1)
+            store_y(g + 1)
+            store_y(g)
+        group_vector(y_bf[0], y_rows4[0], 0, PLANE_VECTOR)
+        group_scalar(y_bf[0], y_rows4[0], PLANE_VECTOR, HALF)
+        group_vector(y_bf[1], y_rows4[1], 0, PLANE_VECTOR)
+        group_scalar(y_bf[1], y_rows4[1], PLANE_VECTOR, HALF)
+        quantize_y(0)
         store_words(0)
-        cast_vector(y_bf[1], y_rows4[1], 0, PLANE_VECTOR)
-        nc.scalar.copy(out=walk_out(y_bf[1], PLANE_VECTOR, HALF), in_=walk_in(y_rows4[1], PLANE_VECTOR, HALF))
-        quantize(y_codes[1][:], y_scales[:, HALF:N], y_bf[1][:])
+        quantize_y(1)
         store_words(1)
         for q in range(G):
             queue = nc.scalar if q % 2 == 0 else nc.sync

from contextlib import ExitStack

import concourse.mybir as mybir

G, D, M, N, L = 4, 128, 128, 512, 768
TAPS = 3
FLOPS = 2 * G * TAPS * D * M * N

F32 = mybir.dt.float32
BF16 = mybir.dt.bfloat16
U32 = mybir.dt.uint32
I32 = mybir.dt.int32
U8 = mybir.dt.uint8
FP8X4 = mybir.dt.float8_e4m3fn_x4
ACT = mybir.ActivationFunctionType
ALU = mybir.AluOpType

P = 128
PACK = 4
ROWS = 32
CHUNK = 128
HALF = 256
X_PARTS = ((0, 512), (512, 640), (640, 768))
X_VECTOR = 344
MIDDLE_VECTOR = 32
LAST_VECTOR = 80
PLANE_VECTOR = 144


def walk_out(t, c0, c1):
    return t[:, c0:c1, :].rearrange("p (c i) t -> p c t i", i=4)


def walk_in(t, c0, c1):
    return t[:, :, c0:c1].rearrange("p t (c i) -> p c t i", i=4)


def tile_rows_pl_conv_relu_kernel(tc, x, w0, w1, w2, b, out_0, out_1, out_2):
    nc = tc.nc
    x_rows = x.rearrange("g (p j) l -> (g p) j l", j=PACK)
    w_rows = [w.rearrange("g (p j) m -> (g p) j m", j=PACK) for w in (w0, w1, w2)]
    words_hbm = out_1.rearrange("s p n u -> (s p) (n u)").bitcast(I32)
    scales_hbm = out_2.rearrange("s f n -> (s f) n").bitcast(I32)

    with ExitStack() as ctx:
        pool = ctx.enter_context(tc.tile_pool(name="sb", bufs=1))
        psum = ctx.enter_context(tc.psum_pool(name="ps", bufs=1))
        ctx.enter_context(tc.manual_schedule())

        def sb(name, shape, dtype):
            return pool.tile(shape, dtype, name=name, align_bytes=64)

        x_width = [l1 - l0 for l0, l1 in X_PARTS]
        x_raw = [sb("x_raw%d" % a, [P, PACK, wd], F32) for a, wd in enumerate(x_width)]
        x_bf = [sb("x_bf%d" % a, [P, wd, PACK], BF16) for a, wd in enumerate(x_width)]
        x_codes = [sb("x_codes%d" % a, [P, wd], U32) for a, wd in enumerate(x_width)]
        x_scales = [sb("x_scales%d" % a, [P, wd], U8) for a, wd in enumerate(x_width)]
        w_raw = [sb("w_raw%d" % t, [P, PACK, M], F32) for t in range(TAPS)]
        w_bf = [sb("w_bf%d" % t, [P, M, PACK], BF16) for t in range(TAPS)]
        w_codes = [sb("w_codes%d" % t, [P, M], U32) for t in range(TAPS)]
        w_scales = [sb("w_scales%d" % t, [P, M], U8) for t in range(TAPS)]
        b_rows = sb("b_rows", [P, G * ROWS], F32)
        b_cols = sb("b_cols", [P, G * ROWS], F32)
        acc = [[psum.tile([P, HALF], F32, name="acc%d_%d" % (h, g)) for g in range(G)] for h in range(2)]
        y32 = [sb("y32_%d" % g, [P, N], F32) for g in range(G)]
        y16 = [[sb("y16_%d_%d" % (h, g), [P, HALF], BF16) for g in range(G)] for h in range(2)]
        y_rows4 = [sb("y_rows4_%d" % h, [P, PACK, HALF], BF16) for h in range(2)]
        y_bf = [sb("y_bf%d" % h, [P, HALF, PACK], BF16) for h in range(2)]
        y_codes = [sb("y_codes%d" % h, [P, HALF], U32) for h in range(2)]
        y_scales = sb("y_scales", [P, N], U8)

        def quantize(codes, scales, grouped):
            nc.vector.quantize_mx(
                out=codes.bitcast(FP8X4), scales=scales, in_=grouped.rearrange("p w j -> p (w j)")
            )

        def quantize_x(a, c0, c1):
            quantize(x_codes[a][:, c0:c1], x_scales[a][:, c0:c1], x_bf[a][:, c0:c1, :])

        def quantize_w(t):
            quantize(w_codes[t][:], w_scales[t][:], w_bf[t][:])

        def quantize_y(h):
            quantize(y_codes[h][:], y_scales[:, h * HALF : (h + 1) * HALF], y_bf[h][:])

        def group_vector(dst, src, c0, c1):
            nc.vector.tensor_copy(out=walk_out(dst, c0, c1), in_=walk_in(src, c0, c1))

        def group_scalar(dst, src, c0, c1):
            nc.scalar.activation(out=walk_out(dst, c0, c1), in_=walk_in(src, c0, c1), func=ACT.Copy)

        def tap(j, t):
            h, l0 = j // 2, (j + t) * CHUNK
            a = max(a for a in range(len(X_PARTS)) if X_PARTS[a][0] <= l0)
            c0 = l0 - X_PARTS[a][0]
            for g in range(G):
                rows = slice(ROWS * g, ROWS * (g + 1))
                nc.tensor.matmul_mx(
                    out=acc[h][g][:, (j % 2) * CHUNK : (j % 2 + 1) * CHUNK],
                    lhsT=w_codes[t][rows, :].bitcast(FP8X4),
                    lhsT_scale=w_scales[t][rows, :],
                    rhs=x_codes[a][rows, c0 : c0 + CHUNK].bitcast(FP8X4),
                    rhs_scale=x_scales[a][rows, c0 : c0 + CHUNK],
                    start=(t == 0),
                    stop=(t == TAPS - 1),
                )

        def relu_scalar(dst, h, g):
            nc.scalar.activation(
                out=dst, in_=acc[h][g][:], func=ACT.Relu, bias=b_cols[:, ROWS * g : ROWS * g + 1]
            )

        def relu_vector(dst, h, g):
            nc.vector.tensor_scalar(
                out=dst, in0=acc[h][g][:], scalar1=b_cols[:, ROWS * g : ROWS * g + 1], scalar2=0.0,
                op0=ALU.add, op1=ALU.max,
            )

        def y32_half(h, g):
            return y32[g][:, h * HALF : (h + 1) * HALF]

        def regroup(queue, h, g):
            queue.dma_start(out=y_rows4[h][ROWS * g : ROWS * (g + 1), :, :], in_=y16[h][g][:])

        def store_y(g):
            nc.sync.dma_start(out=out_0[M * g : M * (g + 1), :], in_=y32[g][:])

        def store_words(h):
            nc.sync.dma_start(out=words_hbm[:, h * HALF : (h + 1) * HALF], in_=y_codes[h][:].bitcast(I32))

        def load_x(a):
            nc.sync.dma_start(out=x_raw[a][:], in_=x_rows[:, :, X_PARTS[a][0] : X_PARTS[a][1]])

        load_x(0)
        nc.vector.memset(b_rows[:], 0.0)
        nc.sync.dma_start(
            out=b_rows[0:P:ROWS, :].rearrange("a (g i) -> a g i", g=G),
            in_=b.rearrange("g (a i) o -> a g (i o)", i=ROWS),
        )
        for t in range(TAPS):
            nc.sync.dma_start(out=w_raw[t][:], in_=w_rows[t])
        load_x(1)
        load_x(2)

        group_scalar(x_bf[0], x_raw[0], X_VECTOR, x_width[0])
        group_vector(x_bf[0], x_raw[0], 0, HALF)
        group_vector(x_bf[0], x_raw[0], HALF, X_VECTOR)
        group_scalar(w_bf[0], w_raw[0], 0, M)
        group_scalar(w_bf[1], w_raw[1], 0, M)
        quantize_x(0, 0, HALF)
        quantize_x(0, HALF, x_width[0])
        quantize_w(0)
        tap(0, 0)
        tap(2, 0)
        group_vector(w_bf[2], w_raw[2], 0, M)
        quantize_w(1)
        tap(0, 1)
        tap(2, 1)
        quantize_w(2)
        tap(0, 2)
        for t in range(TAPS):
            tap(1, t)

        group_vector(x_bf[1], x_raw[1], 0, MIDDLE_VECTOR)
        group_scalar(x_bf[1], x_raw[1], MIDDLE_VECTOR, CHUNK)
        nc.vector.transpose(out=b_cols[:], in_=b_rows[:])
        quantize_x(1, 0, CHUNK)
        tap(2, 2)
        tap(3, 0)
        tap(3, 1)

        group_vector(x_bf[2], x_raw[2], 0, LAST_VECTOR)
        group_scalar(x_bf[2], x_raw[2], LAST_VECTOR, CHUNK)
        quantize_x(2, 0, CHUNK)
        tap(3, 2)
        for g in (0, 1):
            relu_scalar(y16[0][g][:], 0, g)
            regroup(nc.sync, 0, g)
        relu_vector(y16[0][3][:], 0, 3)
        regroup(nc.sync, 0, 3)
        relu_scalar(y16[0][2][:], 0, 2)
        regroup(nc.sync, 0, 2)

        relu_scalar(y16[1][0][:], 1, 0)
        relu_vector(y16[1][1][:], 1, 1)
        regroup(nc.sync, 1, 0)
        regroup(nc.sync, 1, 1)
        relu_scalar(y16[1][2][:], 1, 2)
        relu_vector(y16[1][3][:], 1, 3)
        regroup(nc.scalar, 1, 2)
        regroup(nc.sync, 1, 3)
        for g in (0, 2):
            for h in range(2):
                relu_scalar(y32_half(h, g), h, g)
                relu_vector(y32_half(h, g + 1), h, g + 1)
            store_y(g + 1)
            store_y(g)
        group_vector(y_bf[0], y_rows4[0], 0, PLANE_VECTOR)
        group_scalar(y_bf[0], y_rows4[0], PLANE_VECTOR, HALF)
        group_vector(y_bf[1], y_rows4[1], 0, PLANE_VECTOR)
        group_scalar(y_bf[1], y_rows4[1], PLANE_VECTOR, HALF)
        quantize_y(0)
        store_words(0)
        quantize_y(1)
        store_words(1)
        for q in range(G):
            queue = nc.scalar if q % 2 == 0 else nc.sync
            queue.dma_start(
                out=scales_hbm[4 * q : 4 * q + 4, :], in_=y_scales[ROWS * q : ROWS * q + 4, :].bitcast(I32)
            )
